import numpy as np
import ml_dtypes


def mxq(x, axis, fmt="e4m3"):
    dtype, down = {"e4m3": (ml_dtypes.float8_e4m3fn, 7), "e5m2": (ml_dtypes.float8_e5m2, 14)}[fmt]
    v = np.moveaxis(np.asarray(x, np.float32).astype(ml_dtypes.bfloat16).astype(np.float64), axis, -1)
    blocks = v.reshape(v.shape[:-1] + (-1, 32))
    amax = np.abs(blocks).max(-1, keepdims=True)
    byte = np.maximum(np.where(amax > 0, np.frexp(amax)[1] - 1 + 127, 0) - down, 1)
    scale = np.exp2(byte - 127.0)
    codes = (blocks / scale).astype(np.float32).astype(dtype).astype(np.float64)
    return np.moveaxis((codes * scale).reshape(v.shape), -1, axis)


WIDE = False


def mx_kscale(k):
    if not WIDE:
        return np.ones(k)
    levels = np.array([10, -10, 5, -5, 0])
    if k % 512:
        return np.exp2(np.random.permutation(np.resize(levels, k // 32))).repeat(32)
    a = np.empty((k // 512, 16))
    for p in range(k // 512):
        a[p, :8] = np.random.permutation(np.resize(levels, 8))
        for g in range(8):
            far = levels[np.abs(levels - a[p, g]) >= 10]
            a[p, g + 8] = far[np.random.randint(len(far))]
    return np.exp2(a.ravel()).repeat(32)


def f64(x):
    return np.asarray(x).astype(np.float64)


def striped8(idx):
    return np.asarray(idx).reshape(8, -1, 16).transpose(0, 2, 1).reshape(128, -1).astype(np.uint16)


def unstriped8(offs):
    return offs.reshape(8, 16, -1).transpose(0, 2, 1).reshape(8, -1).astype(np.int64)


def pick8(x, idx, run):
    r = np.arange(len(x))
    return x[r[:, None], idx[r % (8 * run) // run]]


E2M1 = np.array([0.0, 0.5, 1.0, 1.5, 2.0, 3.0, 4.0, 6.0, -0.0, -0.5, -1.0, -1.5, -2.0, -3.0, -4.0, -6.0])


def pack_weight(w, fmt):
    k, n = w.shape
    w = f64(np.asarray(w, np.float32).astype(ml_dtypes.bfloat16)).reshape(k // 32, 32, n)
    amax = np.abs(w).max(1)
    if fmt == "e4m3":
        byte = np.frexp(amax)[1] - 1 + 127 - 7
    else:
        mant, ex = np.frexp(amax / 6.0)
        byte = np.where(mant > 0.5, ex, ex - 1) + 127
    byte = np.clip(np.where(amax > 0, byte, 1), 1, 254)
    scaled = (w * np.exp2(127.0 - byte)[:, None, :]).reshape(k, n).astype(np.float32)
    by_word = np.ascontiguousarray(scaled.reshape(k // 512, 128, 4, n).transpose(0, 1, 3, 2))
    if fmt == "e4m3":
        words = by_word.astype(ml_dtypes.float8_e4m3fn).view(np.uint8)
    else:
        c = by_word.astype(ml_dtypes.float4_e2m1fn).view(np.uint8) & 0xF
        words = (c[..., 0::2] | (c[..., 1::2] << 4)).reshape(k // 512, 128, 2 * n)
    return np.ascontiguousarray(words), np.ascontiguousarray(byte.astype(np.uint8).reshape(k // 512, 16, n))


def unpack_weight(words, scales, fmt):
    g, _, n = scales.shape
    words = np.ascontiguousarray(words).reshape(g, 128, n, -1)
    if fmt == "e4m3":
        vals = words.view(ml_dtypes.float8_e4m3fn).astype(np.float64)
    else:
        nib = np.empty((g, 128, n, 4), np.uint8)
        nib[..., 0::2] = words & 0xF
        nib[..., 1::2] = words >> 4
        vals = E2M1[nib]
    vals = vals * np.repeat(np.exp2(scales.astype(np.float64) - 127.0), 8, axis=1)[..., None]
    return vals.transpose(0, 1, 3, 2).reshape(g * 512, n)


D, T, I, Q, G = 512, 1024, 512, 128, 64


def setup_inputs():
    n = np.random.standard_normal
    idx = np.stack([np.random.permutation(T)[:I] for _ in range(8)])
    idx2 = np.stack([np.random.permutation(T)[:I] for _ in range(8)])
    fd = mx_kscale(D)
    keysp = pack_weight(n((D, T)) / fd[:, None], "e4m3")
    return {
        "query": (n((D, Q)) * 0.9 / np.sqrt(D) * fd[:, None]).astype(np.float32),
        "query2": (n((D, Q)) * 0.9 / np.sqrt(D) * fd[:, None]).astype(np.float32),
        "keys_words": keysp[0],
        "keys_scales": keysp[1],
        "lam": (np.random.uniform(0.8, 1.6, (Q, 1))).astype(np.float32),
        "reserve": (np.random.uniform(20.0, 60.0, (Q, 1))).astype(np.float32),
        "old": (np.random.uniform(0.0, 2.0, (Q, T))).astype(np.float32),
        "fade": (np.random.uniform(0.3, 0.9, (Q, 1))).astype(np.float32),
        "offs": striped8(idx),
        "offs2": striped8(idx2),
    }


def reference(query, query2, keys_words, keys_scales, lam, reserve, old, fade, offs, offs2):
    idx = unstriped8(offs)
    idx2 = unstriped8(offs2)
    keysu = unpack_weight(keys_words, keys_scales, "e4m3")
    queryq = mxq(f64(query), 0, "e4m3")
    a = queryq.T @ keysu
    query2q = mxq(f64(query2), 0, "e4m3")
    b = query2q.T @ keysu
    s = np.log(np.exp(pick8(a, idx, 16)) + np.exp(pick8(b, idx2, 16))) * f64(lam)
    p = np.exp(s)
    pg = p.reshape(Q, G, I // G).sum(axis=2)
    pr = np.repeat(pg, I // G, axis=1)
    r = p / (pr - p)
    w = r / (np.sum(r, axis=1, keepdims=True) + f64(reserve))
    ws = w * 256.0
    wf = np.zeros((Q, T))
    wf[np.arange(Q)[:, None], idx[np.arange(Q) % 128 // 16]] = ws
    y = f64(old) * f64(fade) + wf
    return y

@@ -1,0 +1,230 @@
+import math
+from contextlib import ExitStack
+
+import concourse.mybir as mybir
+
+D, T, SLOTS, Q, RUN = 512, 1024, 512, 128, 8
+FLOPS = 2 * 2 * D * Q * T
+
+F32 = mybir.dt.float32
+BF16 = mybir.dt.bfloat16
+I32 = mybir.dt.int32
+U32 = mybir.dt.uint32
+U16 = mybir.dt.uint16
+U8 = mybir.dt.uint8
+FP8X4 = mybir.dt.float8_e4m3fn_x4
+ALU = mybir.AluOpType
+ACT = mybir.ActivationFunctionType
+AXIS = mybir.AxisListType
+
+P = 128
+PACK = 4
+BANK = 512
+CAP = 2.0**60
+LOG_CAP = 60.0 * math.log(2.0)
+HALVES = ((0, 256), (256, 512))
+PIECES = ((0, 128), (128, 256), (256, 512))
+
+
+def tile_attend_eithertoken_oddsof_counts_heads_kernel(
+    tc, query, query2, keys_words, keys_scales, lam, reserve, old, fade, offs, offs2, out
+):
+    nc = tc.nc
+    with ExitStack() as ctx:
+        keep = ctx.enter_context(tc.tile_pool(name="keep", bufs=1))
+        psum = ctx.enter_context(tc.psum_pool(name="psum", bufs=1))
+
+        staged = keep.tile([4, 4, T // 4], I32, name="staged")
+        nc.scalar.dma_start(out=staged[:], in_=keys_scales[0].bitcast(I32).rearrange("(a r) c -> r a c", r=4))
+        raws = [keep.tile([P, PACK, Q], F32, name="raw%d" % s, tag="raw_old%d" % s) for s in range(2)]
+        words = [keep.tile([P, BANK], U32, name="words%d" % h, align_bytes=64) for h in range(2)]
+        key_bytes = keys_words[0].rearrange("p n t -> p (n t)")
+        nc.sync.dma_start(out=raws[0][:], in_=query.rearrange("(p j) q -> p j q", j=PACK))
+        nc.sync.dma_start(out=words[0][:].bitcast(I32), in_=key_bytes[:, : BANK * PACK].bitcast(I32))
+        nc.sync.dma_start(out=words[1][:].bitcast(I32), in_=key_bytes[:, BANK * PACK :].bitcast(I32))
+        nc.sync.dma_start(out=raws[1][:], in_=query2.rearrange("(p j) q -> p j q", j=PACK))
+        list_a = keep.tile([P, SLOTS // 16], U16, name="list_a")
+        list_b = keep.tile([P, SLOTS // 16], U16, name="list_b")
+        nc.sync.dma_start(list_a[:], offs)
+        nc.sync.dma_start(list_b[:], offs2)
+        lam_col = keep.tile([P, 1], F32, name="lam_col")
+        reserve_col = keep.tile([P, 1], F32, name="reserve_col")
+        fade_col = keep.tile([P, 1], F32, name="fade_col")
+        nc.sync.dma_start(out=lam_col[:], in_=lam)
+        nc.sync.dma_start(out=fade_col[:], in_=fade)
+        nc.sync.dma_start(out=reserve_col[:], in_=reserve)
+
+        key_scales = keep.tile([P, T], U8, name="key_scales", align_bytes=64)
+        nc.vector.memset(key_scales[:].bitcast(I32), 0)
+        for a in range(4):
+            nc.vector.tensor_copy(out=key_scales[32 * a : 32 * a + 4, :].bitcast(I32), in_=staged[:, a, :])
+        placed = keep.tile([P, T], F32, name="placed")
+        nc.gpsimd.memset(placed[:], 0.0)
+
+        codes, scales = [], []
+        for s in range(2):
+            grouped = keep.tile([P, Q, PACK], BF16, name="grouped%d" % s, tag="grouped", align_bytes=64)
+            woven = grouped[:].rearrange("p (c i) t -> p c t i", i=4)
+            rows = raws[s][:].rearrange("p t (c i) -> p c t i", i=4)
+            if s == 0:
+                nc.vector.tensor_copy(out=woven[:, :20], in_=rows[:, :20])
+                nc.scalar.activation(woven[:, 20:], rows[:, 20:], ACT.Copy)
+            else:
+                nc.vector.tensor_copy(out=woven, in_=rows)
+            code = keep.tile([P, Q], U32, name="codes%d" % s, align_bytes=64)
+            scale = keep.tile([P, Q], U8, name="scales%d" % s, align_bytes=64)
+            nc.vector.quantize_mx(
+                out=code[:].bitcast(FP8X4), scales=scale[:], in_=grouped[:].rearrange("p q t -> p (q t)")
+            )
+            codes.append(code)
+            scales.append(scale)
+
+        olds = []
+        for h in range(2):
+            old_half = keep.tile([P, BANK], F32, name="old%d" % h, tag="raw_old%d" % h)
+            nc.sync.dma_start(out=old_half[:], in_=old[:, h * BANK : (h + 1) * BANK])
+            olds.append(old_half)
+
+        scores = []
+        for s in range(2):
+            score = keep.tile([P, T], F32, name="score%d" % s)
+            for h in range(2):
+                bank = psum.tile([P, BANK], F32, name="bank%d%d" % (s, h))
+                nc.tensor.matmul_mx(
+                    out=bank[:],
+                    lhsT=codes[s][:].bitcast(FP8X4),
+                    lhsT_scale=scales[s][:],
+                    rhs=words[h][:].bitcast(FP8X4),
+                    rhs_scale=key_scales[:, h * BANK : (h + 1) * BANK],
+                    start=True,
+                    stop=True,
+                )
+                if (s, h) == (0, 0):
+                    nc.scalar.copy(out=score[:, :BANK], in_=bank[:])
+                else:
+                    nc.vector.tensor_copy(out=score[:, h * BANK : (h + 1) * BANK], in_=bank[:])
+            scores.append(score)
+
+        first = keep.tile([P, SLOTS], F32, name="first")
+        lead = keep.tile([P, SLOTS], F32, name="lead")
+        ratio = keep.tile([P, SLOTS], F32, name="ratio")
+        capped = keep.tile([P, SLOTS], F32, name="capped")
+        beyond = keep.tile([P, SLOTS], F32, name="beyond")
+        first_lam = keep.tile([P, SLOTS], F32, name="first_lam")
+        base = keep.tile([P, SLOTS], F32, name="base")
+        nc.scalar.activation(first[:], scores[0][:].indirect(list_a[:]), ACT.Copy)
+        for lo, hi in HALVES:
+            nc.vector.tensor_tensor(
+                lead[:, lo:hi], scores[1][:].indirect(list_b[:, lo // 16 : hi // 16]), first[:, lo:hi], ALU.subtract
+            )
+            nc.scalar.activation(ratio[:, lo:hi], lead[:, lo:hi], ACT.Exp)
+        nc.vector.tensor_scalar(beyond[:], lead[:], LOG_CAP, 0.0, ALU.subtract, ALU.max)
+        nc.vector.tensor_scalar_mul(first_lam[:], first[:], lam_col[:])
+        nc.vector.tensor_scalar_min(capped[:], ratio[:], CAP)
+        nc.vector.scalar_tensor_tensor(base[:], beyond[:], lam_col[:], first_lam[:], ALU.mult, ALU.add)
+
+        logs = keep.tile([P, SLOTS], F32, name="logs")
+        slot_score = keep.tile([P, SLOTS], F32, name="slot_score")
+        run_top = keep.tile([P, SLOTS // RUN], F32, name="run_top")
+        below = keep.tile([P, SLOTS], F32, name="below")
+        p = keep.tile([P, SLOTS], F32, name="p")
+        pairs = keep.tile([P, SLOTS // 2], F32, name="pairs")
+        quads = keep.tile([P, SLOTS // 4], F32, name="quads")
+        other6 = keep.tile([P, SLOTS // 2], F32, name="other6")
+        other7 = keep.tile([P, SLOTS], F32, name="other7", tag="other_faded0")
+
+        for lo, hi in HALVES:
+            nc.scalar.activation(logs[:, lo:hi], capped[:, lo:hi], ACT.Ln, bias=1.0)
+        for lo, hi in HALVES:
+            nc.vector.scalar_tensor_tensor(
+                slot_score[:, lo:hi], logs[:, lo:hi], lam_col[:], base[:, lo:hi], ALU.mult, ALU.add
+            )
+        for lo, hi in HALVES:
+            nc.vector.tensor_reduce(
+                run_top[:, lo // RUN : hi // RUN], slot_score[:, lo:hi].rearrange("p (g i) -> p g i", i=RUN),
+                AXIS.X, ALU.max,
+            )
+        for lo, hi in HALVES:
+            runs = (hi - lo) // RUN
+            nc.vector.tensor_tensor(
+                below[:, lo:hi].rearrange("p (g i) -> p g i", i=RUN),
+                slot_score[:, lo:hi].rearrange("p (g i) -> p g i", i=RUN),
+                run_top[:, lo // RUN : hi // RUN].unsqueeze(2).broadcast_to([P, runs, RUN]),
+                ALU.subtract,
+            )
+        for lo, hi in HALVES:
+            nc.scalar.activation(p[:, lo:hi], below[:, lo:hi], ACT.Exp)
+        for lo, hi in HALVES:
+            by2 = p[:, lo:hi].rearrange("p (n j) -> p n j", j=2)
+            nc.vector.tensor_tensor(pairs[:, lo // 2 : hi // 2], by2[:, :, 0], by2[:, :, 1], ALU.add)
+        for lo, hi in HALVES:
+            by2 = pairs[:, lo // 2 : hi // 2].rearrange("p (n j) -> p n j", j=2)
+            nc.vector.tensor_tensor(quads[:, lo // 4 : hi // 4], by2[:, :, 0], by2[:, :, 1], ALU.add)
+        for lo, hi in HALVES:
+            runs = (hi - lo) // RUN
+            nc.vector.tensor_tensor(
+                other6[:, lo // 2 : hi // 2].rearrange("p (g m j) -> p g m j", m=2, j=2),
+                pairs[:, lo // 2 : hi // 2].rearrange("p (g m j) -> p g m j", m=2, j=2)[:, :, :, ::-1],
+                quads[:, lo // 4 : hi // 4].rearrange("p (g m) -> p g m", m=2)[:, :, ::-1]
+                .unsqueeze(3).broadcast_to([P, runs, 2, 2]),
+                ALU.add,
+            )
+        for lo, hi in HALVES:
+            nc.vector.tensor_tensor(
+                other7[:, lo:hi].rearrange("p (n j) -> p n j", j=2),
+                p[:, lo:hi].rearrange("p (n j) -> p n j", j=2)[:, :, ::-1],
+                other6[:, lo // 2 : hi // 2].unsqueeze(2).broadcast_to([P, (hi - lo) // 2, 2]),
+                ALU.add,
+            )
+
+        root = keep.tile([P, SLOTS], F32, name="root", tag="other_faded1")
+        inverse = keep.tile([P, SLOTS], F32, name="inverse")
+        odds = keep.tile([P, SLOTS], F32, name="odds")
+        sums = keep.tile([P, len(PIECES)], F32, name="sums")
+        def invert(lo, hi):
+            nc.scalar.activation(root[:, lo:hi], other7[:, lo:hi], ACT.Abs_reciprocal_sqrt)
+
+        def square(lo, hi):
+            nc.scalar.activation(inverse[:, lo:hi], root[:, lo:hi], ACT.Square)
+
+        def weigh(k):
+            lo, hi = PIECES[k]
+            nc.vector.scalar_tensor_tensor(
+                odds[:, lo:hi], p[:, lo:hi], 256.0, inverse[:, lo:hi], ALU.mult, ALU.mult, accum_out=sums[:, k : k + 1]
+            )
+
+        def put(lo, hi):
+            nc.vector.tensor_copy(placed[:].indirect(list_a[:, lo // 16 : hi // 16]), odds[:, lo:hi])
+
+        invert(*PIECES[0])
+        invert(*PIECES[1])
+        square(*PIECES[0])
+        square(*PIECES[1])
+        invert(*PIECES[2])
+        square(*PIECES[2])
+        weigh(0)
+        weigh(1)
+        put(*PIECES[0])
+        weigh(2)
+        put(PIECES[1][0], SLOTS)
+        parts = keep.tile([P, len(PIECES)], F32, name="parts")
+        total = keep.tile([P, 1], F32, name="total")
+        norm_root = keep.tile([P, 1], F32, name="norm_root")
+        norm = keep.tile([P, 1], F32, name="norm")
+        nc.scalar.activation(parts[:], sums[:], ACT.Copy, accum_out=total[:])
+        nc.scalar.activation(norm_root[:], total[:], ACT.Abs_reciprocal_sqrt, bias=reserve_col[:], scale=1.0 / 256.0)
+        nc.scalar.activation(norm[:], norm_root[:], ACT.Square)
+
+        fadeds = []
+        for h in range(2):
+            faded = keep.tile([P, BANK], F32, name="faded%d" % h, tag="other_faded%d" % h)
+            nc.scalar.activation(faded[:], olds[h][:], ACT.Copy, scale=fade_col[:])
+            fadeds.append(faded)
+        for k in range(4):
+            h, lo = divmod(k * 256, BANK)
+            result = keep.tile([P, 256], F32, name="result%d" % k)
+            nc.vector.scalar_tensor_tensor(
+                result[:], placed[:, k * 256 : (k + 1) * 256], norm[:], fadeds[h][:, lo : lo + 256], ALU.mult, ALU.add
+            )
+            queue = nc.sync if k % 2 == 0 else nc.scalar
+            queue.dma_start(out=out[:, k * 256 : (k + 1) * 256], in_=result[:])

@@ -20,9 +20,11 @@ AXIS = mybir.AxisListType
 P = 128
 PACK = 4
 BANK = 512
+PASS = 256
 CAP = 2.0**60
 LOG_CAP = 60.0 * math.log(2.0)
 HALVES = ((0, 256), (256, 512))
+STORES = ((0, 256), (256, 512), (512, 832), (832, 1024))
 PIECES = ((0, 128), (128, 256), (256, 512))
 
 
@@ -41,8 +43,8 @@ def tile_attend_eithertoken_oddsof_counts_heads_kernel(
         key_bytes = keys_words[0].rearrange("p n t -> p (n t)")
         nc.sync.dma_start(out=raws[0][:], in_=query.rearrange("(p j) q -> p j q", j=PACK))
         nc.sync.dma_start(out=words[0][:].bitcast(I32), in_=key_bytes[:, : BANK * PACK].bitcast(I32))
-        nc.sync.dma_start(out=words[1][:].bitcast(I32), in_=key_bytes[:, BANK * PACK :].bitcast(I32))
         nc.sync.dma_start(out=raws[1][:], in_=query2.rearrange("(p j) q -> p j q", j=PACK))
+        nc.sync.dma_start(out=words[1][:].bitcast(I32), in_=key_bytes[:, BANK * PACK :].bitcast(I32))
         list_a = keep.tile([P, SLOTS // 16], U16, name="list_a")
         list_b = keep.tile([P, SLOTS // 16], U16, name="list_b")
         nc.sync.dma_start(list_a[:], offs)
@@ -50,27 +52,23 @@ def tile_attend_eithertoken_oddsof_counts_heads_kernel(
         lam_col = keep.tile([P, 1], F32, name="lam_col")
         reserve_col = keep.tile([P, 1], F32, name="reserve_col")
         fade_col = keep.tile([P, 1], F32, name="fade_col")
-        nc.sync.dma_start(out=lam_col[:], in_=lam)
-        nc.sync.dma_start(out=fade_col[:], in_=fade)
-        nc.sync.dma_start(out=reserve_col[:], in_=reserve)
+        nc.gpsimd.dma_start(out=lam_col[:], in_=lam)
+        nc.gpsimd.dma_start(out=fade_col[:], in_=fade)
+        nc.gpsimd.dma_start(out=reserve_col[:], in_=reserve)
 
         key_scales = keep.tile([P, T], U8, name="key_scales", align_bytes=64)
         nc.vector.memset(key_scales[:].bitcast(I32), 0)
         for a in range(4):
             nc.vector.tensor_copy(out=key_scales[32 * a : 32 * a + 4, :].bitcast(I32), in_=staged[:, a, :])
         placed = keep.tile([P, T], F32, name="placed")
-        nc.gpsimd.memset(placed[:], 0.0)
+        nc.vector.memset(placed[:], 0.0)
 
         codes, scales = [], []
         for s in range(2):
-            grouped = keep.tile([P, Q, PACK], BF16, name="grouped%d" % s, tag="grouped", align_bytes=64)
+            grouped = keep.tile([P, Q, PACK], BF16, name="grouped%d" % s, align_bytes=64)
             woven = grouped[:].rearrange("p (c i) t -> p c t i", i=4)
             rows = raws[s][:].rearrange("p t (c i) -> p c t i", i=4)
-            if s == 0:
-                nc.vector.tensor_copy(out=woven[:, :20], in_=rows[:, :20])
-                nc.scalar.activation(woven[:, 20:], rows[:, 20:], ACT.Copy)
-            else:
-                nc.vector.tensor_copy(out=woven, in_=rows)
+            nc.scalar.activation(woven, rows, ACT.Copy)
             code = keep.tile([P, Q], U32, name="codes%d" % s, align_bytes=64)
             scale = keep.tile([P, Q], U8, name="scales%d" % s, align_bytes=64)
             nc.vector.quantize_mx(
@@ -88,21 +86,22 @@ def tile_attend_eithertoken_oddsof_counts_heads_kernel(
         scores = []
         for s in range(2):
             score = keep.tile([P, T], F32, name="score%d" % s)
-            for h in range(2):
-                bank = psum.tile([P, BANK], F32, name="bank%d%d" % (s, h))
+            for lo in range(0, T, PASS):
+                h, at = divmod(lo, BANK)
+                bank = psum.tile([P, PASS], F32, name="bank%d_%d" % (s, lo))
                 nc.tensor.matmul_mx(
                     out=bank[:],
                     lhsT=codes[s][:].bitcast(FP8X4),
                     lhsT_scale=scales[s][:],
-                    rhs=words[h][:].bitcast(FP8X4),
-                    rhs_scale=key_scales[:, h * BANK : (h + 1) * BANK],
+                    rhs=words[h][:, at : at + PASS].bitcast(FP8X4),
+                    rhs_scale=key_scales[:, lo : lo + PASS],
                     start=True,
                     stop=True,
                 )
-                if (s, h) == (0, 0):
-                    nc.scalar.copy(out=score[:, :BANK], in_=bank[:])
+                if s == 0 and at == 0:
+                    nc.scalar.copy(out=score[:, lo : lo + PASS], in_=bank[:])
                 else:
-                    nc.vector.tensor_copy(out=score[:, h * BANK : (h + 1) * BANK], in_=bank[:])
+                    nc.vector.tensor_copy(out=score[:, lo : lo + PASS], in_=bank[:])
             scores.append(score)
 
         first = keep.tile([P, SLOTS], F32, name="first")
@@ -113,15 +112,16 @@ def tile_attend_eithertoken_oddsof_counts_heads_kernel(
         first_lam = keep.tile([P, SLOTS], F32, name="first_lam")
         base = keep.tile([P, SLOTS], F32, name="base")
         nc.scalar.activation(first[:], scores[0][:].indirect(list_a[:]), ACT.Copy)
+        second = keep.tile([P, 256], F32, name="second")
+        nc.vector.tensor_tensor(lead[:, :256], scores[1][:].indirect(list_b[:, :16]), first[:, :256], ALU.subtract)
+        nc.scalar.activation(second[:], scores[1][:].indirect(list_b[:, 16:]), ACT.Copy)
+        nc.vector.tensor_tensor(lead[:, 256:], second[:], first[:, 256:], ALU.subtract)
         for lo, hi in HALVES:
-            nc.vector.tensor_tensor(
-                lead[:, lo:hi], scores[1][:].indirect(list_b[:, lo // 16 : hi // 16]), first[:, lo:hi], ALU.subtract
-            )
             nc.scalar.activation(ratio[:, lo:hi], lead[:, lo:hi], ACT.Exp)
         nc.vector.tensor_scalar(beyond[:], lead[:], LOG_CAP, 0.0, ALU.subtract, ALU.max)
-        nc.vector.tensor_scalar_mul(first_lam[:], first[:], lam_col[:])
         nc.vector.tensor_scalar_min(capped[:], ratio[:], CAP)
-        nc.vector.scalar_tensor_tensor(base[:], beyond[:], lam_col[:], first_lam[:], ALU.mult, ALU.add)
+        nc.vector.tensor_tensor(first_lam[:], beyond[:], first[:], ALU.add)
+        nc.vector.tensor_scalar_mul(base[:], first_lam[:], lam_col[:])
 
         logs = keep.tile([P, SLOTS], F32, name="logs")
         slot_score = keep.tile([P, SLOTS], F32, name="slot_score")
@@ -131,7 +131,8 @@ def tile_attend_eithertoken_oddsof_counts_heads_kernel(
         pairs = keep.tile([P, SLOTS // 2], F32, name="pairs")
         quads = keep.tile([P, SLOTS // 4], F32, name="quads")
         other6 = keep.tile([P, SLOTS // 2], F32, name="other6")
-        other7 = keep.tile([P, SLOTS], F32, name="other7", tag="other_faded0")
+        other7 = keep.tile([P, SLOTS], F32, name="other7")
+        against = keep.tile([P, SLOTS], F32, name="against", tag="other_faded0")
 
         for lo, hi in HALVES:
             nc.scalar.activation(logs[:, lo:hi], capped[:, lo:hi], ACT.Ln, bias=1.0)
@@ -154,6 +155,8 @@ def tile_attend_eithertoken_oddsof_counts_heads_kernel(
             )
         for lo, hi in HALVES:
             nc.scalar.activation(p[:, lo:hi], below[:, lo:hi], ACT.Exp)
+        p_inverse = keep.tile([P, SLOTS], F32, name="p_inverse")
+        nc.scalar.activation(p_inverse[:], below[:], ACT.Exp, scale=-1.0)
         for lo, hi in HALVES:
             by2 = p[:, lo:hi].rearrange("p (n j) -> p n j", j=2)
             nc.vector.tensor_tensor(pairs[:, lo // 2 : hi // 2], by2[:, :, 0], by2[:, :, 1], ALU.add)
@@ -176,36 +179,32 @@ def tile_attend_eithertoken_oddsof_counts_heads_kernel(
                 other6[:, lo // 2 : hi // 2].unsqueeze(2).broadcast_to([P, (hi - lo) // 2, 2]),
                 ALU.add,
             )
+        for lo, hi in HALVES:
+            nc.vector.scalar_tensor_tensor(
+                against[:, lo:hi], p_inverse[:, lo:hi], 2.0**100, other7[:, lo:hi], ALU.min, ALU.mult
+            )
 
         root = keep.tile([P, SLOTS], F32, name="root", tag="other_faded1")
-        inverse = keep.tile([P, SLOTS], F32, name="inverse")
         odds = keep.tile([P, SLOTS], F32, name="odds")
         sums = keep.tile([P, len(PIECES)], F32, name="sums")
-        def invert(lo, hi):
-            nc.scalar.activation(root[:, lo:hi], other7[:, lo:hi], ACT.Abs_reciprocal_sqrt)
-
-        def square(lo, hi):
-            nc.scalar.activation(inverse[:, lo:hi], root[:, lo:hi], ACT.Square)
-
-        def weigh(k):
+        def invert(k):
             lo, hi = PIECES[k]
-            nc.vector.scalar_tensor_tensor(
-                odds[:, lo:hi], p[:, lo:hi], 256.0, inverse[:, lo:hi], ALU.mult, ALU.mult, accum_out=sums[:, k : k + 1]
-            )
+            nc.scalar.activation(root[:, lo:hi], against[:, lo:hi], ACT.Abs_reciprocal_sqrt)
+
+        def square(k):
+            lo, hi = PIECES[k]
+            nc.scalar.activation(odds[:, lo:hi], root[:, lo:hi], ACT.Square, scale=16.0, accum_out=sums[:, k : k + 1])
 
         def put(lo, hi):
             nc.vector.tensor_copy(placed[:].indirect(list_a[:, lo // 16 : hi // 16]), odds[:, lo:hi])
 
-        invert(*PIECES[0])
-        invert(*PIECES[1])
-        square(*PIECES[0])
-        square(*PIECES[1])
-        invert(*PIECES[2])
-        square(*PIECES[2])
-        weigh(0)
-        weigh(1)
+        invert(0)
+        invert(1)
+        square(0)
         put(*PIECES[0])
-        weigh(2)
+        square(1)
+        invert(2)
+        square(2)
         put(PIECES[1][0], SLOTS)
         parts = keep.tile([P, len(PIECES)], F32, name="parts")
         total = keep.tile([P, 1], F32, name="total")
@@ -220,11 +219,11 @@ def tile_attend_eithertoken_oddsof_counts_heads_kernel(
             faded = keep.tile([P, BANK], F32, name="faded%d" % h, tag="other_faded%d" % h)
             nc.scalar.activation(faded[:], olds[h][:], ACT.Copy, scale=fade_col[:])
             fadeds.append(faded)
-        for k in range(4):
-            h, lo = divmod(k * 256, BANK)
-            result = keep.tile([P, 256], F32, name="result%d" % k)
+        for k, (lo, hi) in enumerate(STORES):
+            h = lo // BANK
+            result = keep.tile([P, hi - lo], F32, name="result%d" % k)
             nc.vector.scalar_tensor_tensor(
-                result[:], placed[:, k * 256 : (k + 1) * 256], norm[:], fadeds[h][:, lo : lo + 256], ALU.mult, ALU.add
+                result[:], placed[:, lo:hi], norm[:], fadeds[h][:, lo - h * BANK : hi - h * BANK], ALU.mult, ALU.add
             )
             queue = nc.sync if k % 2 == 0 else nc.scalar
-            queue.dma_start(out=out[:, k * 256 : (k + 1) * 256], in_=result[:])
+            queue.dma_start(out=out[:, lo:hi], in_=result[:])

import math
from contextlib import ExitStack

import concourse.mybir as mybir

D, T, SLOTS, Q, RUN = 512, 1024, 512, 128, 8
FLOPS = 2 * 2 * D * Q * T

F32 = mybir.dt.float32
BF16 = mybir.dt.bfloat16
I32 = mybir.dt.int32
U32 = mybir.dt.uint32
U16 = mybir.dt.uint16
U8 = mybir.dt.uint8
FP8X4 = mybir.dt.float8_e4m3fn_x4
ALU = mybir.AluOpType
ACT = mybir.ActivationFunctionType
AXIS = mybir.AxisListType

P = 128
PACK = 4
BANK = 512
PASS = 256
CAP = 2.0**60
LOG_CAP = 60.0 * math.log(2.0)
HALVES = ((0, 256), (256, 512))
STORES = ((0, 256), (256, 512), (512, 832), (832, 1024))
PIECES = ((0, 128), (128, 256), (256, 512))


def tile_attend_eithertoken_oddsof_counts_heads_kernel(
    tc, query, query2, keys_words, keys_scales, lam, reserve, old, fade, offs, offs2, out
):
    nc = tc.nc
    with ExitStack() as ctx:
        keep = ctx.enter_context(tc.tile_pool(name="keep", bufs=1))
        psum = ctx.enter_context(tc.psum_pool(name="psum", bufs=1))

        staged = keep.tile([4, 4, T // 4], I32, name="staged")
        nc.scalar.dma_start(out=staged[:], in_=keys_scales[0].bitcast(I32).rearrange("(a r) c -> r a c", r=4))
        raws = [keep.tile([P, PACK, Q], F32, name="raw%d" % s, tag="raw_old%d" % s) for s in range(2)]
        words = [keep.tile([P, BANK], U32, name="words%d" % h, align_bytes=64) for h in range(2)]
        key_bytes = keys_words[0].rearrange("p n t -> p (n t)")
        nc.sync.dma_start(out=raws[0][:], in_=query.rearrange("(p j) q -> p j q", j=PACK))
        nc.sync.dma_start(out=words[0][:].bitcast(I32), in_=key_bytes[:, : BANK * PACK].bitcast(I32))
        nc.sync.dma_start(out=raws[1][:], in_=query2.rearrange("(p j) q -> p j q", j=PACK))
        nc.sync.dma_start(out=words[1][:].bitcast(I32), in_=key_bytes[:, BANK * PACK :].bitcast(I32))
        list_a = keep.tile([P, SLOTS // 16], U16, name="list_a")
        list_b = keep.tile([P, SLOTS // 16], U16, name="list_b")
        nc.sync.dma_start(list_a[:], offs)
        nc.sync.dma_start(list_b[:], offs2)
        lam_col = keep.tile([P, 1], F32, name="lam_col")
        reserve_col = keep.tile([P, 1], F32, name="reserve_col")
        fade_col = keep.tile([P, 1], F32, name="fade_col")
        nc.gpsimd.dma_start(out=lam_col[:], in_=lam)
        nc.gpsimd.dma_start(out=fade_col[:], in_=fade)
        nc.gpsimd.dma_start(out=reserve_col[:], in_=reserve)

        key_scales = keep.tile([P, T], U8, name="key_scales", align_bytes=64)
        nc.vector.memset(key_scales[:].bitcast(I32), 0)
        for a in range(4):
            nc.vector.tensor_copy(out=key_scales[32 * a : 32 * a + 4, :].bitcast(I32), in_=staged[:, a, :])
        placed = keep.tile([P, T], F32, name="placed")
        nc.vector.memset(placed[:], 0.0)

        codes, scales = [], []
        for s in range(2):
            grouped = keep.tile([P, Q, PACK], BF16, name="grouped%d" % s, align_bytes=64)
            woven = grouped[:].rearrange("p (c i) t -> p c t i", i=4)
            rows = raws[s][:].rearrange("p t (c i) -> p c t i", i=4)
            nc.scalar.activation(woven, rows, ACT.Copy)
            code = keep.tile([P, Q], U32, name="codes%d" % s, align_bytes=64)
            scale = keep.tile([P, Q], U8, name="scales%d" % s, align_bytes=64)
            nc.vector.quantize_mx(
                out=code[:].bitcast(FP8X4), scales=scale[:], in_=grouped[:].rearrange("p q t -> p (q t)")
            )
            codes.append(code)
            scales.append(scale)

        olds = []
        for h in range(2):
            old_half = keep.tile([P, BANK], F32, name="old%d" % h, tag="raw_old%d" % h)
            nc.sync.dma_start(out=old_half[:], in_=old[:, h * BANK : (h + 1) * BANK])
            olds.append(old_half)

        scores = []
        for s in range(2):
            score = keep.tile([P, T], F32, name="score%d" % s)
            for lo in range(0, T, PASS):
                h, at = divmod(lo, BANK)
                bank = psum.tile([P, PASS], F32, name="bank%d_%d" % (s, lo))
                nc.tensor.matmul_mx(
                    out=bank[:],
                    lhsT=codes[s][:].bitcast(FP8X4),
                    lhsT_scale=scales[s][:],
                    rhs=words[h][:, at : at + PASS].bitcast(FP8X4),
                    rhs_scale=key_scales[:, lo : lo + PASS],
                    start=True,
                    stop=True,
                )
                if s == 0 and at == 0:
                    nc.scalar.copy(out=score[:, lo : lo + PASS], in_=bank[:])
                else:
                    nc.vector.tensor_copy(out=score[:, lo : lo + PASS], in_=bank[:])
            scores.append(score)

        first = keep.tile([P, SLOTS], F32, name="first")
        lead = keep.tile([P, SLOTS], F32, name="lead")
        ratio = keep.tile([P, SLOTS], F32, name="ratio")
        capped = keep.tile([P, SLOTS], F32, name="capped")
        beyond = keep.tile([P, SLOTS], F32, name="beyond")
        first_lam = keep.tile([P, SLOTS], F32, name="first_lam")
        base = keep.tile([P, SLOTS], F32, name="base")
        nc.scalar.activation(first[:], scores[0][:].indirect(list_a[:]), ACT.Copy)
        second = keep.tile([P, 256], F32, name="second")
        nc.vector.tensor_tensor(lead[:, :256], scores[1][:].indirect(list_b[:, :16]), first[:, :256], ALU.subtract)
        nc.scalar.activation(second[:], scores[1][:].indirect(list_b[:, 16:]), ACT.Copy)
        nc.vector.tensor_tensor(lead[:, 256:], second[:], first[:, 256:], ALU.subtract)
        for lo, hi in HALVES:
            nc.scalar.activation(ratio[:, lo:hi], lead[:, lo:hi], ACT.Exp)
        nc.vector.tensor_scalar(beyond[:], lead[:], LOG_CAP, 0.0, ALU.subtract, ALU.max)
        nc.vector.tensor_scalar_min(capped[:], ratio[:], CAP)
        nc.vector.tensor_tensor(first_lam[:], beyond[:], first[:], ALU.add)
        nc.vector.tensor_scalar_mul(base[:], first_lam[:], lam_col[:])

        logs = keep.tile([P, SLOTS], F32, name="logs")
        slot_score = keep.tile([P, SLOTS], F32, name="slot_score")
        run_top = keep.tile([P, SLOTS // RUN], F32, name="run_top")
        below = keep.tile([P, SLOTS], F32, name="below")
        p = keep.tile([P, SLOTS], F32, name="p")
        pairs = keep.tile([P, SLOTS // 2], F32, name="pairs")
        quads = keep.tile([P, SLOTS // 4], F32, name="quads")
        other6 = keep.tile([P, SLOTS // 2], F32, name="other6")
        other7 = keep.tile([P, SLOTS], F32, name="other7")
        against = keep.tile([P, SLOTS], F32, name="against", tag="other_faded0")

        for lo, hi in HALVES:
            nc.scalar.activation(logs[:, lo:hi], capped[:, lo:hi], ACT.Ln, bias=1.0)
        for lo, hi in HALVES:
            nc.vector.scalar_tensor_tensor(
                slot_score[:, lo:hi], logs[:, lo:hi], lam_col[:], base[:, lo:hi], ALU.mult, ALU.add
            )
        for lo, hi in HALVES:
            nc.vector.tensor_reduce(
                run_top[:, lo // RUN : hi // RUN], slot_score[:, lo:hi].rearrange("p (g i) -> p g i", i=RUN),
                AXIS.X, ALU.max,
            )
        for lo, hi in HALVES:
            runs = (hi - lo) // RUN
            nc.vector.tensor_tensor(
                below[:, lo:hi].rearrange("p (g i) -> p g i", i=RUN),
                slot_score[:, lo:hi].rearrange("p (g i) -> p g i", i=RUN),
                run_top[:, lo // RUN : hi // RUN].unsqueeze(2).broadcast_to([P, runs, RUN]),
                ALU.subtract,
            )
        for lo, hi in HALVES:
            nc.scalar.activation(p[:, lo:hi], below[:, lo:hi], ACT.Exp)
        p_inverse = keep.tile([P, SLOTS], F32, name="p_inverse")
        nc.scalar.activation(p_inverse[:], below[:], ACT.Exp, scale=-1.0)
        for lo, hi in HALVES:
            by2 = p[:, lo:hi].rearrange("p (n j) -> p n j", j=2)
            nc.vector.tensor_tensor(pairs[:, lo // 2 : hi // 2], by2[:, :, 0], by2[:, :, 1], ALU.add)
        for lo, hi in HALVES:
            by2 = pairs[:, lo // 2 : hi // 2].rearrange("p (n j) -> p n j", j=2)
            nc.vector.tensor_tensor(quads[:, lo // 4 : hi // 4], by2[:, :, 0], by2[:, :, 1], ALU.add)
        for lo, hi in HALVES:
            runs = (hi - lo) // RUN
            nc.vector.tensor_tensor(
                other6[:, lo // 2 : hi // 2].rearrange("p (g m j) -> p g m j", m=2, j=2),
                pairs[:, lo // 2 : hi // 2].rearrange("p (g m j) -> p g m j", m=2, j=2)[:, :, :, ::-1],
                quads[:, lo // 4 : hi // 4].rearrange("p (g m) -> p g m", m=2)[:, :, ::-1]
                .unsqueeze(3).broadcast_to([P, runs, 2, 2]),
                ALU.add,
            )
        for lo, hi in HALVES:
            nc.vector.tensor_tensor(
                other7[:, lo:hi].rearrange("p (n j) -> p n j", j=2),
                p[:, lo:hi].rearrange("p (n j) -> p n j", j=2)[:, :, ::-1],
                other6[:, lo // 2 : hi // 2].unsqueeze(2).broadcast_to([P, (hi - lo) // 2, 2]),
                ALU.add,
            )
        for lo, hi in HALVES:
            nc.vector.scalar_tensor_tensor(
                against[:, lo:hi], p_inverse[:, lo:hi], 2.0**100, other7[:, lo:hi], ALU.min, ALU.mult
            )

        root = keep.tile([P, SLOTS], F32, name="root", tag="other_faded1")
        odds = keep.tile([P, SLOTS], F32, name="odds")
        sums = keep.tile([P, len(PIECES)], F32, name="sums")
        def invert(k):
            lo, hi = PIECES[k]
            nc.scalar.activation(root[:, lo:hi], against[:, lo:hi], ACT.Abs_reciprocal_sqrt)

        def square(k):
            lo, hi = PIECES[k]
            nc.scalar.activation(odds[:, lo:hi], root[:, lo:hi], ACT.Square, scale=16.0, accum_out=sums[:, k : k + 1])

        def put(lo, hi):
            nc.vector.tensor_copy(placed[:].indirect(list_a[:, lo // 16 : hi // 16]), odds[:, lo:hi])

        invert(0)
        invert(1)
        square(0)
        put(*PIECES[0])
        square(1)
        invert(2)
        square(2)
        put(PIECES[1][0], SLOTS)
        parts = keep.tile([P, len(PIECES)], F32, name="parts")
        total = keep.tile([P, 1], F32, name="total")
        norm_root = keep.tile([P, 1], F32, name="norm_root")
        norm = keep.tile([P, 1], F32, name="norm")
        nc.scalar.activation(parts[:], sums[:], ACT.Copy, accum_out=total[:])
        nc.scalar.activation(norm_root[:], total[:], ACT.Abs_reciprocal_sqrt, bias=reserve_col[:], scale=1.0 / 256.0)
        nc.scalar.activation(norm[:], norm_root[:], ACT.Square)

        fadeds = []
        for h in range(2):
            faded = keep.tile([P, BANK], F32, name="faded%d" % h, tag="other_faded%d" % h)
            nc.scalar.activation(faded[:], olds[h][:], ACT.Copy, scale=fade_col[:])
            fadeds.append(faded)
        for k, (lo, hi) in enumerate(STORES):
            h = lo // BANK
            result = keep.tile([P, hi - lo], F32, name="result%d" % k)
            nc.vector.scalar_tensor_tensor(
                result[:], placed[:, lo:hi], norm[:], fadeds[h][:, lo - h * BANK : hi - h * BANK], ALU.mult, ALU.add
            )
            queue = nc.sync if k % 2 == 0 else nc.scalar
            queue.dma_start(out=out[:, lo:hi], in_=result[:])
